import numpy as np
import ml_dtypes


def mxq(x, axis, fmt="e4m3"):
    dtype, down = {"e4m3": (ml_dtypes.float8_e4m3fn, 7), "e5m2": (ml_dtypes.float8_e5m2, 14)}[fmt]
    v = np.moveaxis(np.asarray(x, np.float32).astype(ml_dtypes.bfloat16).astype(np.float64), axis, -1)
    blocks = v.reshape(v.shape[:-1] + (-1, 32))
    amax = np.abs(blocks).max(-1, keepdims=True)
    byte = np.maximum(np.where(amax > 0, np.frexp(amax)[1] - 1 + 127, 0) - down, 1)
    scale = np.exp2(byte - 127.0)
    codes = (blocks / scale).astype(np.float32).astype(dtype).astype(np.float64)
    return np.moveaxis((codes * scale).reshape(v.shape), -1, axis)


WIDE = False


def mx_kscale(k):
    if not WIDE:
        return np.ones(k)
    levels = np.array([10, -10, 5, -5, 0])
    if k % 512:
        return np.exp2(np.random.permutation(np.resize(levels, k // 32))).repeat(32)
    a = np.empty((k // 512, 16))
    for p in range(k // 512):
        a[p, :8] = np.random.permutation(np.resize(levels, 8))
        for g in range(8):
            far = levels[np.abs(levels - a[p, g]) >= 10]
            a[p, g + 8] = far[np.random.randint(len(far))]
    return np.exp2(a.ravel()).repeat(32)


def f64(x):
    return np.asarray(x).astype(np.float64)


def striped(idx):
    return np.tile(idx.reshape(-1, 16).T, (8, 1)).astype(np.uint16)


def unstriped(offs):
    return offs[:16].T.reshape(-1).astype(np.int64)


def striped8(idx):
    return np.concatenate([x.reshape(-1, 16).T for x in idx]).astype(np.uint16)


def runs(offs, k):
    lists = np.stack([offs[16 * r : 16 * r + 16].T.reshape(-1) for r in range(8)]).astype(np.int64)
    return lists[np.arange(k) % 512 // 64]


def pack_weight(w):
    k, n = w.shape
    w = f64(np.asarray(w, np.float32).astype(ml_dtypes.bfloat16)).reshape(k // 32, 32, n)
    amax = np.abs(w).max(1)
    byte = np.clip(np.where(amax > 0, np.frexp(amax)[1] - 1 + 127 - 7, 1), 1, 254)
    scaled = (w * np.exp2(127.0 - byte)[:, None, :]).reshape(k, n).astype(np.float32)
    words = np.ascontiguousarray(scaled.reshape(k // 512, 128, 4, n).transpose(0, 1, 3, 2)).astype(ml_dtypes.float8_e4m3fn).view(np.uint8)
    return words, np.ascontiguousarray(byte.astype(np.uint8).reshape(k // 512, 16, n))


def unpack_weight(words, scales):
    g, p, n, _ = words.shape
    vals = np.ascontiguousarray(words).view(ml_dtypes.float8_e4m3fn).astype(np.float64) * np.repeat(np.exp2(scales.astype(np.float64) - 127.0), 8, axis=1)[..., None]
    return vals.transpose(0, 1, 3, 2).reshape(g * 512, n)


def sigmoid(v):
    return 1.0 / (1.0 + np.exp(-np.maximum(v, -700.0)))

def planes(y):
    n, m = y.shape
    v = y.astype(np.float32).astype(ml_dtypes.bfloat16).astype(np.float64).reshape(n // 32, 32, m)
    top = np.abs(v).max(1)
    byte = np.clip(np.where(top > 0, np.frexp(top)[1] - 1 + 127 - 7, 1), 1, 254)
    codes = (v * np.exp2(127.0 - byte)[:, None, :]).reshape(n, m).astype(np.float32).astype(ml_dtypes.float8_e4m3fn).view(np.uint8)
    words = codes.reshape(n // 512, 128, 4, m).transpose(0, 1, 3, 2)
    return np.ascontiguousarray(words), np.ascontiguousarray(byte.astype(np.uint8).reshape(n // 512, 16, m))


K, T, S, G, H, C = 512, 1024, 512, 2048, 512, 512


def setup_inputs():
    n = np.random.standard_normal
    s = mx_kscale(K)[:, None]
    packed_xT = pack_weight(n((K, T)) * s)
    packed_dT = pack_weight(n((K, G)) / s)
    return {
        "x_words": packed_xT[0],
        "x_scales": packed_xT[1],
        "d_words": packed_dT[0],
        "d_scales": packed_dT[1],
        "gs": (np.random.uniform(0.5, 1.5, (K, 1)) / s).astype(np.float32),
        "offs": striped(np.random.permutation(T)[:S]),
        "k1": striped8(np.random.randint(0, G, (8, H))),
        "n1": striped(np.random.permutation(S)),
        "n2": striped(np.random.permutation(S)),
        "cand": striped(np.random.permutation(T)[:C]),
        "two": striped(np.random.permutation(T)[:S]),
        "k2": striped8(np.random.randint(0, G, (8, H))),
        "n3": striped8(np.stack([np.random.permutation(S) for _ in range(8)])),
        "n4": striped8(np.stack([np.random.permutation(S) for _ in range(8)])),
    }


def reference(x_words, x_scales, d_words, d_scales, gs, offs, k1, n1, n2, cand, two, k2, n3, n4):
    x_cand = unpack_weight(x_words, x_scales)[:, unstriped(cand)]
    d_k1 = unpack_weight(d_words, d_scales)[np.arange(K)[:, None], runs(k1, K)]
    xq = unpack_weight(x_words, x_scales)[:, unstriped(offs)]
    h = 0.0625 * (d_k1.T @ xq)
    sm = np.maximum(h, h[:, unstriped(n2)])
    ds = np.zeros((H, S))
    ds[:, unstriped(n1)] = sm
    z = f64(gs) * (ds * sigmoid(h))
    a = 0.0625 * ((x_cand.T @ mxq(z, 0, "e4m3")))
    d_k2 = unpack_weight(d_words, d_scales)[np.arange(K)[:, None], runs(k2, K)]
    x_two = unpack_weight(x_words, x_scales)[:, unstriped(two)]
    b = 0.0625 * (d_k2.T @ x_two)
    out_0 = a[np.arange(C)[:, None], runs(n3, C)] - (np.tanh(b) * (b[np.arange(H)[:, None], runs(n4, H)]))
    return (out_0,) + planes(out_0)

from contextlib import ExitStack

import concourse.mybir as mybir

F32 = mybir.dt.float32
BF16 = mybir.dt.bfloat16
I32 = mybir.dt.int32
U32 = mybir.dt.uint32
U16 = mybir.dt.uint16
U8 = mybir.dt.uint8
FP8X4 = mybir.dt.float8_e4m3fn_x4
ACT = mybir.ActivationFunctionType
ALU = mybir.AluOpType

P = 128
PACK = 4
N = 512
HALF = N // 2
T = 1024
G = 2048
SIXTEENTH = 0.0625
FLOPS = 3 * 2 * 512 * 512 * 512


def tile_picked_pqcjsoftbsendg_none_po_kernel(
    tc, x_words, x_scales, d_words, d_scales, gs, offs, k1, n1, n2, cand, two, k2, n3, n4, out_0, out_1, out_2
):
    nc = tc.nc
    with ExitStack() as ctx:
        keep = ctx.enter_context(tc.tile_pool(name="keep", bufs=1))
        psum = ctx.enter_context(tc.psum_pool(name="psum", bufs=1))

        def load_list(ap, name):
            t = keep.tile([P, N // 16], U16, name=name)
            nc.sync.dma_start(t[:], ap)
            return t

        def half(lst, u):
            return lst[:, u * (HALF // 16) : (u + 1) * (HALF // 16)]

        def cols(u):
            return slice(u * HALF, (u + 1) * HALF)

        ds_tab = keep.tile([P, G], U8, name="ds_tab", align_bytes=64)
        xs_tab = keep.tile([P, T], U8, name="xs_tab", align_bytes=64)
        dw_tab = keep.tile([P, G], U32, name="dw_tab", align_bytes=64)
        xw_tab = keep.tile([P, T], U32, name="xw_tab", align_bytes=64)
        placed_h = keep.tile([P, 2 * N], U8, name="placed_h", align_bytes=64)
        placed_r = keep.tile([P, 3 * N], U8, name="placed_r", align_bytes=64)
        nc.gpsimd.memset(ds_tab[:].bitcast(I32), 0)
        nc.vector.memset(xs_tab[:].bitcast(I32), 0)
        nc.gpsimd.memset(placed_h[:].bitcast(I32), 0)
        nc.gpsimd.memset(placed_r[:].bitcast(I32), 0)

        k1_t = load_list(k1, "k1_t")
        nc.sync.dma_start(ds_tab[:].bitcast(I32)[0:P:8, :], d_scales[0].bitcast(I32))
        offs_t = load_list(offs, "offs_t")
        nc.sync.dma_start(xs_tab[:].bitcast(I32)[0:P:8, :], x_scales[0].bitcast(I32))
        nc.sync.dma_start(dw_tab[:].bitcast(I32), d_words[0].rearrange("p n t -> p (n t)").bitcast(I32))
        nc.sync.dma_start(xw_tab[:].bitcast(I32), x_words[0].rearrange("p n t -> p (n t)").bitcast(I32))

        def gather(dst, table, lst):
            nc.vector.tensor_copy(dst, table[:].indirect(lst[:]))

        def place(dst, src):
            for r in range(PACK):
                nc.sync.dma_start(dst[:].bitcast(I32)[r:P:32, :], src[:].bitcast(I32)[8 * r : P : 32, :])

        def deal_words(src, name):
            dst = keep.tile([P, N], U32, name=name, align_bytes=64)
            nc.vector.tensor_copy(
                dst[:].bitcast(I32).rearrange("p (t c i) -> p c t i", t=PACK, i=4),
                src[:].bitcast(I32).rearrange("p (c i t) -> p c t i", t=PACK, i=4),
            )
            return dst

        def deal_bytes(src, name):
            dst = keep.tile([P, N], U8, name=name, align_bytes=64)
            nc.vector.tensor_copy(
                dst[:].rearrange("p (t c i) -> p c t i", t=PACK, i=16),
                src.rearrange("p (c i t) -> p c t i", t=PACK, i=16),
            )
            return dst

        def words(table, lst, name):
            dst = keep.tile([P, N], U32, name=name, align_bytes=64)
            gather(dst[:], table, lst)
            return dst

        def product(bank, w, s, t, rhs, rhs_scale):
            m = slice(P * t, P * (t + 1))
            nc.tensor.matmul_mx(
                out=bank, lhsT=w[:, m].bitcast(FP8X4), lhsT_scale=s[:, m],
                rhs=rhs.bitcast(FP8X4), rhs_scale=rhs_scale, start=True, stop=True,
            )

        picked_h = keep.tile([P, 2 * N], U8, name="picked_h", align_bytes=64)
        gather(picked_h[:, 0:N], ds_tab, k1_t)
        gather(picked_h[:, N : 2 * N], xs_tab, offs_t)
        place(placed_h, picked_h)
        dw1 = words(dw_tab, k1_t, "dw1")
        xw_offs = words(xw_tab, offs_t, "xw_offs")
        dw1_dealt = deal_words(dw1, "dw1_dealt")
        ds1_dealt = deal_bytes(placed_h[:, 0:N], "ds1_dealt")

        n2_t = load_list(n2, "n2_t")
        k2_t = load_list(k2, "k2_t")
        two_t = load_list(two, "two_t")
        cand_t = load_list(cand, "cand_t")
        n1_t = load_list(n1, "n1_t")
        gs_t = keep.tile([P, PACK], F32, name="gs_t")
        nc.sync.dma_start(gs_t[:], gs.rearrange("(p t) o -> p (t o)", t=PACK))
        n4_t = load_list(n4, "n4_t")
        n3_t = load_list(n3, "n3_t")

        h_banks = [psum.tile([P, N], F32, name=f"h_bank{t}", tag=f"bankA{t}") for t in range(PACK)]
        for t in range(PACK):
            product(h_banks[t][:], dw1_dealt, ds1_dealt, t, xw_offs[:], placed_h[:, N : 2 * N])

        h = [keep.tile([P, N + 16], F32, name=f"h{t}") for t in range(PACK)]
        hg = [keep.tile([P, N], F32, name=f"hg{t}") for t in range(PACK)]
        sm = [keep.tile([P, N], F32, name=f"sm{t}") for t in range(PACK)]
        sig = [keep.tile([P, N], F32, name=f"sig{t}") for t in range(PACK)]
        ds = [keep.tile([P, 704 if t == 3 else N], F32, name=f"ds{t}") for t in range(PACK)]
        nc.scalar.activation(sig[0][:], h_banks[0][:], ACT.Sigmoid, scale=SIXTEENTH)
        for t in range(PACK):
            nc.scalar.activation(h[t][:, 0:N], h_banks[t][:], ACT.Copy, scale=SIXTEENTH)
            nc.scalar.activation(hg[t][:], h[t][:].indirect(n2_t[:]), ACT.Copy)
            nc.vector.tensor_tensor(sm[t][:], hg[t][:], h[t][:, 0:N], ALU.max)

        picked_r = keep.tile([P, 3 * N], U8, name="picked_r", align_bytes=64)
        gather(picked_r[:, 0:N], ds_tab, k2_t)
        gather(picked_r[:, N : 2 * N], xs_tab, cand_t)
        gather(picked_r[:, 2 * N : 3 * N], xs_tab, two_t)
        place(placed_r, picked_r)
        w_r = keep.tile([P, 2 * N], U32, name="w_r", align_bytes=64)
        gather(w_r[:, 0:N], dw_tab, k2_t)
        gather(w_r[:, N : 2 * N], xw_tab, cand_t)
        xw_two = words(xw_tab, two_t, "xw_two")
        w_r_dealt = keep.tile([P, 2 * N], U32, name="w_r_dealt", align_bytes=64)
        s_r_dealt = keep.tile([P, 2 * N], U8, name="s_r_dealt", align_bytes=64)
        nc.vector.tensor_copy(
            w_r_dealt[:].bitcast(I32).rearrange("p (g t c i) -> p g c t i", g=2, t=PACK, i=4),
            w_r[:].bitcast(I32).rearrange("p (g c i t) -> p g c t i", g=2, t=PACK, i=4),
        )
        nc.vector.tensor_copy(
            s_r_dealt[:].rearrange("p (g t c i) -> p g c t i", g=2, t=PACK, i=16),
            placed_r[:, 0 : 2 * N].rearrange("p (g c i t) -> p g c t i", g=2, t=PACK, i=16),
        )
        dw2_dealt = w_r_dealt[:, 0:N]
        xwc_dealt = w_r_dealt[:, N : 2 * N]
        ds2_dealt = s_r_dealt[:, 0:N]
        xsc_dealt = s_r_dealt[:, N : 2 * N]

        for t in range(1, PACK):
            nc.scalar.activation(sig[t][:], h_banks[t][:], ACT.Sigmoid, scale=SIXTEENTH)

        for u in range(2):
            for t in (0, 1):
                nc.scalar.activation(ds[t][:].indirect(half(n1_t, u)), sm[t][:, cols(u)], ACT.Copy)
        nc.vector.tensor_copy(ds[2][:].indirect(half(n1_t, 0)), sm[2][:, cols(0)])
        nc.vector.tensor_copy(ds[3][:].indirect(n1_t[:]), sm[3][:])
        nc.scalar.activation(ds[2][:].indirect(half(n1_t, 1)), sm[2][:, cols(1)], ACT.Copy)

        z_rows = keep.tile([P, PACK, N], BF16, name="z_rows", align_bytes=64)
        for t in (0, 1, 3, 2):
            nc.vector.scalar_tensor_tensor(z_rows[:, t, :], ds[t][:, 0:N], gs_t[:, t : t + 1], sig[t][:], ALU.mult, ALU.mult)
        z_words = keep.tile([P, N], U32, name="z_words", align_bytes=64)
        z_scales = keep.tile([P, N], U8, name="z_scales", align_bytes=64)
        z_grouped = [keep.tile([P, HALF, PACK], BF16, name=f"z_grouped{u}", align_bytes=64) for u in range(2)]
        for u in range(2):
            nc.vector.tensor_copy(
                z_grouped[u][:].rearrange("p (c i) t -> p c t i", i=4),
                z_rows[:, :, cols(u)].rearrange("p t (c i) -> p c t i", i=4),
            )
        for u in range(2):
            nc.vector.quantize_mx(
                out=z_words[:, cols(u)].bitcast(FP8X4), scales=z_scales[:, cols(u)],
                in_=z_grouped[u][:].rearrange("p c t -> p (c t)"),
            )

        b_banks = [psum.tile([P, N], F32, name=f"b_bank{t}", tag=f"bankB{t}") for t in range(PACK)]
        for t in range(PACK):
            product(b_banks[t][:], dw2_dealt, ds2_dealt, t, xw_two[:], placed_r[:, 2 * N : 3 * N])
        b = [keep.tile([P, 2 * N], F32, name=f"b{t}") for t in range(PACK)]
        tanh_b = [keep.tile([P, N], F32, name=f"tanh_b{t}") for t in range(PACK)]
        prod = keep.tile([P, PACK, N], F32, name="prod")
        for t in range(PACK):
            nc.scalar.activation(b[t][:, 0:N], b_banks[t][:], ACT.Copy, scale=SIXTEENTH)
            nc.scalar.activation(tanh_b[t][:], b_banks[t][:], ACT.Tanh, scale=SIXTEENTH)
            nc.vector.tensor_tensor(prod[:, t, :], b[t][:].indirect(n4_t[:]), tanh_b[t][:], ALU.mult)

        a_banks = [psum.tile([P, N], F32, name=f"a_bank{t}", tag=f"bankA{t}") for t in range(PACK)]
        a = [keep.tile([P, N], F32, name=f"a{t}") for t in range(PACK)]
        for t in range(PACK):
            product(a_banks[t][:], xwc_dealt, xsc_dealt, t, z_words[:], z_scales[:])
            nc.scalar.activation(a[t][:], a_banks[t][:], ACT.Copy, scale=SIXTEENTH)
        pieces = [(0, 256), (256, 384), (384, 512)]
        y_words = keep.tile([P, N], U32, name="y_words", align_bytes=64)
        y_scales = keep.tile([P, N], U8, name="y_scales", align_bytes=64)
        out_rows = out_0.rearrange("(p t) j -> p t j", t=PACK)
        out_words = out_1[0].rearrange("p n t -> p (n t)").bitcast(I32)
        for u, (c0, c1) in enumerate(pieces):
            w = c1 - c0
            entries = n3_t[:, c0 // 16 : c1 // 16]
            y = keep.tile([P, PACK, w], F32, name=f"y{u}")
            ag = keep.tile([P, 2, w], F32, name=f"ag{u}")
            y_grouped = keep.tile([P, w, PACK], BF16, name=f"y_grouped{u}", align_bytes=64)
            for t in (2, 3):
                nc.scalar.activation(ag[:, t - 2, :], a[t][:].indirect(entries), ACT.Copy)
            for t in (0, 1):
                nc.vector.tensor_tensor(y[:, t, :], a[t][:].indirect(entries), prod[:, t, c0:c1], ALU.subtract)
            nc.vector.tensor_tensor(y[:, 2:4, :], ag[:], prod[:, 2:4, c0:c1], ALU.subtract)
            nc.sync.dma_start(out_rows[:, :, c0:c1], y[:])
            dst = y_grouped[:].rearrange("p (c i) t -> p c t i", i=4)
            src = y[:].rearrange("p t (c i) -> p c t i", i=4)
            if u < 2:
                nc.scalar.copy(dst, src)
            else:
                nc.vector.tensor_copy(dst, src)
            nc.vector.quantize_mx(
                out=y_words[:, c0:c1].bitcast(FP8X4), scales=y_scales[:, c0:c1],
                in_=y_grouped[:].rearrange("p c t -> p (c t)"),
            )
            nc.sync.dma_start(out_words[:, c0:c1], y_words[:, c0:c1].bitcast(I32))
        for q in range(PACK):
            queue = nc.scalar if q % 2 == 0 else nc.sync
            queue.dma_start(out_2[0].bitcast(I32)[4 * q : 4 * q + 4, :], y_scales[:].bitcast(I32)[32 * q : 32 * q + 4, :])
